import numpy as np
import ml_dtypes


def mxq(x, axis, fmt="e4m3"):
    dtype, down = {"e4m3": (ml_dtypes.float8_e4m3fn, 7), "e5m2": (ml_dtypes.float8_e5m2, 14)}[fmt]
    v = np.moveaxis(np.asarray(x, np.float32).astype(ml_dtypes.bfloat16).astype(np.float64), axis, -1)
    blocks = v.reshape(v.shape[:-1] + (-1, 32))
    amax = np.abs(blocks).max(-1, keepdims=True)
    byte = np.maximum(np.where(amax > 0, np.frexp(amax)[1] - 1 + 127, 0) - down, 1)
    scale = np.exp2(byte - 127.0)
    codes = (blocks / scale).astype(np.float32).astype(dtype).astype(np.float64)
    return np.moveaxis((codes * scale).reshape(v.shape), -1, axis)


WIDE = False


def mx_kscale(k):
    if not WIDE:
        return np.ones(k)
    levels = np.array([10, -10, 5, -5, 0])
    if k % 512:
        return np.exp2(np.random.permutation(np.resize(levels, k // 32))).repeat(32)
    a = np.empty((k // 512, 16))
    for p in range(k // 512):
        a[p, :8] = np.random.permutation(np.resize(levels, 8))
        for g in range(8):
            far = levels[np.abs(levels - a[p, g]) >= 10]
            a[p, g + 8] = far[np.random.randint(len(far))]
    return np.exp2(a.ravel()).repeat(32)


def f64(x):
    return np.asarray(x).astype(np.float64)


def striped(idx):
    return np.tile(idx.reshape(-1, 16).T, (8, 1)).astype(np.uint16)


def unstriped(offs):
    return offs[:16].T.reshape(-1).astype(np.int64)


E2M1 = np.array([0.0, 0.5, 1.0, 1.5, 2.0, 3.0, 4.0, 6.0, -0.0, -0.5, -1.0, -1.5, -2.0, -3.0, -4.0, -6.0])


def pack_weight(w, fmt):
    k, n = w.shape
    w = f64(np.asarray(w, np.float32).astype(ml_dtypes.bfloat16)).reshape(k // 32, 32, n)
    amax = np.abs(w).max(1)
    if fmt == "e4m3":
        byte = np.frexp(amax)[1] - 1 + 127 - 7
    else:
        mant, ex = np.frexp(amax / 6.0)
        byte = np.where(mant > 0.5, ex, ex - 1) + 127
    byte = np.clip(np.where(amax > 0, byte, 1), 1, 254)
    scaled = (w * np.exp2(127.0 - byte)[:, None, :]).reshape(k, n).astype(np.float32)
    by_word = np.ascontiguousarray(scaled.reshape(k // 512, 128, 4, n).transpose(0, 1, 3, 2))
    if fmt == "e4m3":
        words = by_word.astype(ml_dtypes.float8_e4m3fn).view(np.uint8)
    else:
        c = by_word.astype(ml_dtypes.float4_e2m1fn).view(np.uint8) & 0xF
        words = (c[..., 0::2] | (c[..., 1::2] << 4)).reshape(k // 512, 128, 2 * n)
    return np.ascontiguousarray(words), np.ascontiguousarray(byte.astype(np.uint8).reshape(k // 512, 16, n))


def unpack_weight(words, scales, fmt):
    g, _, n = scales.shape
    words = np.ascontiguousarray(words).reshape(g, 128, n, -1)
    if fmt == "e4m3":
        vals = words.view(ml_dtypes.float8_e4m3fn).astype(np.float64)
    else:
        nib = np.empty((g, 128, n, 4), np.uint8)
        nib[..., 0::2] = words & 0xF
        nib[..., 1::2] = words >> 4
        vals = E2M1[nib]
    vals = vals * np.repeat(np.exp2(scales.astype(np.float64) - 127.0), 8, axis=1)[..., None]
    return vals.transpose(0, 1, 3, 2).reshape(g * 512, n)


def gelu(v):
    return 0.5 * v * (1.0 + np.tanh(np.sqrt(2.0 / np.pi) * (v + 0.044715 * v**3)))


K, H, T, S, T2, P = 1536, 1024, 2048, 512, 1024, 512

def setup_inputs():
    n = np.random.standard_normal
    s = mx_kscale(K)[:, None]
    u = mx_kscale(H)[:, None]
    tab_words, tab_scales = pack_weight(n((K, T)) * s, "e4m3")
    w4_words, w4_scales = pack_weight(n((K, H)) / np.sqrt(K) / s * u.T, "e2m1")
    return {
        "tab_words": tab_words, "tab_scales": tab_scales,
        "offs": striped(np.random.permutation(T)[:S]),
        "w1": (n((K, H)) / np.sqrt(K) / s * u.T).astype(np.float32),
        "b1": (0.6 * n(H) * u[:, 0]).astype(np.float32),
        "w4_words": w4_words, "w4_scales": w4_scales,
        "page0": (n((H, T2)) * u).astype(np.float32),
        "wgs": np.exp(0.3 * n((128, S))).astype(np.float32),
        "offs2": striped(np.random.permutation(T2)[:S]),
        "offs3": striped(np.random.permutation(T2)[:P]),
        "offs4": striped(np.random.permutation(T2)[:P]),
        "base": (0.6 * n(H) * u[:, 0]).astype(np.float32),
        "rw": (n(H) / np.sqrt(H) / u[:, 0] ** 2).astype(np.float32),
        "pair": (0.7 * n((P, P))).astype(np.float32),
    }

def reference(tab_words, tab_scales, offs, w1, b1, w4_words, w4_scales, page0, wgs,
              offs2, offs3, offs4, base, rw, pair):
    v = unpack_weight(tab_words, tab_scales, "e4m3")[:, unstriped(offs)]
    w4 = unpack_weight(w4_words, w4_scales, "e2m1")
    h1 = (mxq(f64(w1), 0, "e4m3").T @ v) + f64(b1)[:, None]
    h = np.maximum(h1, w4.T @ v)
    page = f64(page0).copy()
    page[:, unstriped(offs2)] = np.tile(f64(wgs), (H // 128, 1)) * h
    x1 = page[:, unstriped(offs3)]
    x2 = np.abs(page[:, unstriped(offs4)] - f64(base)[:, None])
    x2 = x2 * f64(rw)[:, None]
    e = mxq(x1, 0, "e4m3").T @ mxq(x2, 0, "e4m3")
    return np.tanh(e + f64(pair))

@@ -1,0 +1,327 @@
+from contextlib import ExitStack
+
+import concourse.mybir as mybir
+from concourse.masks import make_identity
+
+K, H, T, S, T2, PN = 1536, 1024, 2048, 512, 1024, 512
+FLOPS = 2 * (2 * K * H * S + H * PN * PN)
+
+F32 = mybir.dt.float32
+BF16 = mybir.dt.bfloat16
+I32 = mybir.dt.int32
+U32 = mybir.dt.uint32
+U16 = mybir.dt.uint16
+U8 = mybir.dt.uint8
+FP8X4 = mybir.dt.float8_e4m3fn_x4
+FP4X4 = mybir.dt.float4_e2m1fn_x4
+ALU = mybir.AluOpType
+ACT = mybir.ActivationFunctionType
+
+P = 128
+PASSES = K // 512
+SLICES = H // P
+GROUPS = H // 512
+TILES = PN // P
+W1_CHUNKS = ((0, 1), (1, 2), (2, 3), (3, 4), (4, 6), (6, 8))
+W4_CHUNKS = ((0, 2), (2, 8))
+LATE_PIECES = ((0, 2), (2, 3), (3, 4))
+
+
+def tile_list_anodise_profile_dye_kernel(
+    tc, tab_words, tab_scales, offs, w1, b1, w4_words, w4_scales, page0, wgs, offs2, offs3, offs4, base, rw, pair, out
+):
+    nc = tc.nc
+    with ExitStack() as ctx:
+        lists = ctx.enter_context(tc.tile_pool(name="lists", bufs=1))
+        keep = ctx.enter_context(tc.tile_pool(name="keep", bufs=1))
+        work = ctx.enter_context(tc.tile_pool(name="work", bufs=2))
+        psum = ctx.enter_context(tc.psum_pool(name="psum", bufs=2))
+
+        def load_list(src, name):
+            t = lists.tile([P, S // 16], U16, name=name)
+            nc.sync.dma_start(t[:], src)
+            return t
+
+        ident_f32 = keep.tile([P, P], F32, name="ident_f32")
+        make_identity(nc, ident_f32[:])
+        tab_sc = keep.tile([P, PASSES * T], U8, name="tab_sc")
+        nc.vector.memset(tab_sc[:].bitcast(I32), 0)
+        for q in range(4):
+            (nc.gpsimd if q < 2 else nc.scalar).dma_start(
+                tab_sc[32 * q : 32 * q + 4, :].bitcast(I32).rearrange("r (a t) -> r a t", a=PASSES),
+                tab_scales[:, 4 * q : 4 * q + 4, :].bitcast(I32).rearrange("a r t -> r a t"),
+            )
+        w4_sc = keep.tile([P, PASSES, H], U8, name="w4_sc", align_bytes=64)
+        nc.vector.memset(w4_sc[:].bitcast(I32), 0)
+        for q in range(4):
+            nc.gpsimd.dma_start(
+                w4_sc[32 * q : 32 * q + 4, :, :].bitcast(I32),
+                w4_scales[:, 4 * q : 4 * q + 4, :].bitcast(I32).rearrange("a r n -> r a n"),
+            )
+        rows = keep.tile([P, P], F32, name="rows")
+        nc.vector.memset(rows[:], 0.0)
+        for i, vec in enumerate((b1, base, rw)):
+            (nc.gpsimd if i else nc.scalar).dma_start(rows[SLICES * i : SLICES * (i + 1), :], vec.rearrange("(s p) -> s p", p=P))
+        ident_bf16 = keep.tile([P, P], BF16, name="ident_bf16")
+        make_identity(nc, ident_bf16[:])
+
+        w1_raw = {}
+
+        def load_w1(c):
+            s0, s1 = W1_CHUNKS[c]
+            for a in range(PASSES):
+                raw = keep.tile([P, 4, (s1 - s0) * P], F32, name="w1_raw%d_%d" % (c, a))
+                nc.sync.dma_start(
+                    raw[:], w1[512 * a : 512 * (a + 1), s0 * P : s1 * P].rearrange("(p j) c -> p j c", j=4)
+                )
+                for s in range(s0, s1):
+                    w1_raw[s, a] = raw[:, :, (s - s0) * P : (s - s0 + 1) * P]
+
+        w4_codes = {}
+
+        def load_w4(c):
+            s0, s1 = W4_CHUNKS[c]
+            t = keep.tile([P, PASSES, (s1 - s0) * 2 * P], U8, name="w4_codes%d" % c, align_bytes=64)
+            nc.sync.dma_start(
+                t[:].bitcast(I32),
+                w4_words[:, :, s0 * 2 * P : s1 * 2 * P].bitcast(I32).rearrange("a p n -> p a n"),
+            )
+            for s in range(s0, s1):
+                w4_codes[s] = t[:, :, (s - s0) * 2 * P : (s - s0 + 1) * 2 * P]
+
+        pages = {}
+
+        def load_page(s):
+            t = keep.tile([P, T2], F32, name="page%d" % s)
+            nc.sync.dma_start(t[:], page0[s * P : (s + 1) * P, :])
+            pages[s] = t
+
+        idx = load_list(offs, "idx")
+        idx2 = load_list(offs2, "idx2")
+        idx4 = load_list(offs4, "idx4")
+        idx3 = load_list(offs3, "idx3")
+        load_w4(0)
+        tab = []
+        for a in range(PASSES):
+            t = keep.tile([P, T], U32, name="tab%d" % a)
+            nc.sync.dma_start(t[:].bitcast(I32), tab_words[a].rearrange("p t i -> p (t i)").bitcast(I32))
+            tab.append(t)
+        load_w1(0)
+        load_page(0)
+        wgs_sb = keep.tile([P, S], F32, name="wgs_sb")
+        nc.sync.dma_start(wgs_sb[:], wgs)
+        load_w1(1)
+        load_w1(2)
+        load_page(1)
+        load_w4(1)
+        load_w1(3)
+        load_page(2)
+        load_w1(4)
+        load_page(3)
+        load_page(4)
+        load_w1(5)
+        for s in range(5, SLICES):
+            load_page(s)
+        pair_sb = keep.tile([P, TILES, PN], F32, name="pair_sb")
+        nc.sync.dma_start(pair_sb[:], pair.rearrange("(t p) j -> p t j", p=P))
+
+        cols_ps = psum.tile([P, 4, P], F32, name="t2")
+        nc.tensor.transpose(cols_ps[:, 0, :], rows[:], ident_f32[:])
+        cols = keep.tile([P, 3 * SLICES], F32, name="cols")
+        nc.scalar.copy(cols[:], cols_ps[:, 0, 0 : 3 * SLICES])
+
+        v_codes = []
+        v_scales = []
+        for a in range(PASSES):
+            sc = keep.tile([P, S], U8, name="v_scales%d" % a, align_bytes=64)
+            nc.vector.tensor_copy(sc[:], tab_sc[:, a * T : (a + 1) * T].indirect(idx[:]))
+            v_scales.append(sc)
+            t = keep.tile([P, S], U32, name="v_codes%d" % a, align_bytes=64)
+            nc.vector.tensor_copy(t[:], tab[a][:].indirect(idx[:]))
+            v_codes.append(t)
+
+        w1_q = {}
+
+        def quantize_w1(s, by_pass):
+            grouped = keep.tile([P, PASSES * P * 4], BF16, name="w1_bf", tag="w1_bf%d" % (s % 4), align_bytes=64)
+            codes = keep.tile([P, PASSES * P], U32, name="w1_codes%d" % s, align_bytes=64)
+            scales = keep.tile([P, PASSES * P], U8, name="w1_scales%d" % s, align_bytes=64)
+            for a in range(PASSES):
+                part = grouped[:, a * 4 * P : (a + 1) * 4 * P]
+                nc.scalar.copy(
+                    part.rearrange("p (c i j) -> p c j i", i=4, j=4),
+                    w1_raw[s, a].rearrange("p j (c i) -> p c j i", i=4),
+                )
+                if by_pass:
+                    nc.vector.quantize_mx(
+                        out=codes[:, a * P : (a + 1) * P].bitcast(FP8X4), scales=scales[:, a * P : (a + 1) * P], in_=part
+                    )
+            if not by_pass:
+                nc.vector.quantize_mx(out=codes[:].bitcast(FP8X4), scales=scales[:], in_=grouped[:])
+            w1_q[s] = (codes, scales)
+
+        h_sb = {}
+
+        def make_h(s):
+            h4 = psum.tile([P, S], F32, name="h4")
+            h1 = psum.tile([P, S], F32, name="h1")
+            codes, scales = w1_q[s]
+            for a in range(PASSES):
+                nc.tensor.matmul_mx(
+                    out=h4[:],
+                    lhsT=w4_codes[s][:, a, :].bitcast(FP4X4),
+                    lhsT_scale=w4_sc[:, a, s * P : (s + 1) * P],
+                    rhs=v_codes[a][:].bitcast(FP8X4),
+                    rhs_scale=v_scales[a][:],
+                    start=(a == 0),
+                    stop=(a == PASSES - 1),
+                )
+            for a in range(PASSES):
+                nc.tensor.matmul_mx(
+                    out=h1[:],
+                    lhsT=codes[:, a * P : (a + 1) * P].bitcast(FP8X4),
+                    lhsT_scale=scales[:, a * P : (a + 1) * P],
+                    rhs=v_codes[a][:].bitcast(FP8X4),
+                    rhs_scale=v_scales[a][:],
+                    start=(a == 0),
+                    stop=(a == PASSES - 1),
+                )
+            h4_sb = keep.tile([P, S], F32, name="h4_sb", tag="h4_sb%d" % (s % 4))
+            nc.scalar.copy(h4_sb[:], h4[:])
+            h_tag = "w1_bf%d" % ((s + 1) % 4) if 0 < s < SLICES - 1 else "h%d" % s
+            h = keep.tile([P, S], F32, name="h", tag=h_tag, align_bytes=64)
+            nc.vector.scalar_tensor_tensor(h[:], h1[:], cols[:, s : s + 1], h4_sb[:], ALU.add, ALU.max)
+            h_sb[s] = h
+
+        def scatter(s):
+            nc.vector.tensor_tensor(pages[s][:].indirect(idx2[:]), h_sb[s][:], wgs_sb[:], ALU.mult)
+
+        def turn(blocks, dst, pattern):
+            ps = psum.tile([P, 4 * P], BF16, name="t1")
+            for i, block in enumerate(blocks):
+                nc.tensor.transpose(ps[:, i * P : (i + 1) * P], block, ident_bf16[:])
+            nc.scalar.copy(dst, ps[:].bitcast(F32).rearrange(pattern, b=4, u=2))
+
+        turned = {}
+
+        def turn_slice(x, name, s):
+            g, q = divmod(s, 4)
+            if q == 0:
+                turned[name, g] = keep.tile([P, TILES, 2, P], F32, name="turned_%s%d" % (name, g))
+            turn(
+                [x[:, mt * P : (mt + 1) * P] for mt in range(TILES)],
+                turned[name, g][:, :, :, 32 * q : 32 * (q + 1)],
+                "m (b i u) -> m b u i",
+            )
+
+        def fetch(s):
+            if s == 0:
+                both = keep.tile([P, PN + PN // 2], F32, name="both", tag="w1_bf1", align_bytes=64)
+            else:
+                both = keep.tile([P, PN + PN // 2], F32, name="both", tag="h4_sb%d" % ((s + 1) % 4))
+            dye = both[:, 0:PN]
+            nc.vector.tensor_copy(dye, pages[s][:].indirect(idx4[:]))
+            early = s < 4
+            if early:
+                x1 = both[:, PN:].bitcast(BF16)
+                nc.vector.tensor_copy(x1, pages[s][:].indirect(idx3[:]))
+            dist = work.tile([P, PN], F32, name="dist")
+            nc.scalar.activation(dist[:], dye, ACT.Abs, bias=cols[:, SLICES + s : SLICES + s + 1], scale=-1.0)
+            x2 = work.tile([P, PN], BF16, name="x2")
+            nc.scalar.activation(x2[:], dist[:], ACT.Copy, scale=cols[:, 2 * SLICES + s : 2 * SLICES + s + 1])
+            turn_slice(x2, "x2", s)
+            if early:
+                turn_slice(x1, "x1", s)
+
+        def operand(name):
+            grouped = keep.tile([P, PN * 4], BF16, name="grouped_" + name, tag="grouped_" + name[:2], align_bytes=64)
+            codes = keep.tile([P, PN], U32, name="codes_" + name, align_bytes=64)
+            scales = keep.tile([P, PN], U8, name="scales_" + name, align_bytes=64)
+            return grouped, codes, scales
+
+        def turn_back(src, grouped, t0, t1):
+            n = t1 - t0
+            ps = psum.tile([P, 4, P], F32, name="t2")
+            for j in range(n):
+                for u in range(2):
+                    nc.tensor.transpose(ps[:, 2 * j + u, :], src[:, t0 + j, u, :], ident_f32[:])
+            nc.scalar.copy(
+                grouped[:, t0 * 4 * P : t1 * 4 * P].bitcast(F32).rearrange("p (j m u) -> p j m u", j=n, u=2),
+                ps[:, 0 : 2 * n, :].rearrange("p (j u) m -> p j m u", u=2),
+            )
+
+        def quantize_tiles(op, t0, t1):
+            grouped, codes, scales = op
+            nc.vector.quantize_mx(
+                out=codes[:, t0 * P : t1 * P].bitcast(FP8X4),
+                scales=scales[:, t0 * P : t1 * P],
+                in_=grouped[:, t0 * 4 * P : t1 * 4 * P],
+            )
+
+        x_q = {}
+
+        def quantize_x(name, g):
+            op = operand("%s%d" % (name, g))
+            for half in range(2):
+                turn_back(turned[name, g], op[0], 2 * half, 2 * half + 2)
+            quantize_tiles(op, 0, TILES)
+            x_q[name, g] = op
+
+        quantize_w1(0, True)
+        make_h(0)
+
+        scatter(0)
+        quantize_w1(1, False)
+        fetch(0)
+        quantize_w1(2, False)
+        make_h(1)
+        scatter(1)
+        for s in range(1, SLICES):
+            if s + 2 < SLICES:
+                quantize_w1(s + 2, False)
+            if s + 1 < SLICES:
+                make_h(s + 1)
+            fetch(s)
+            if s + 1 < SLICES:
+                scatter(s + 1)
+            if s == 3:
+                quantize_x("x2", 0)
+                quantize_x("x1", 0)
+
+        late = keep.tile([P, 4, PN], BF16, name="late", tag="h%d" % (SLICES - 1), align_bytes=64)
+        for t0, t1 in LATE_PIECES:
+            for q in range(4):
+                nc.vector.tensor_copy(
+                    late[:, q, t0 * P : t1 * P], pages[4 + q][:].indirect(idx3[:, t0 * P // 16 : t1 * P // 16])
+                )
+        quantize_x("x2", 1)
+        x_q["x1", 1] = operand("x11")
+        turned["x1", 1] = keep.tile([P, TILES, 2, P], F32, name="turned_x11")
+        for mt in range(TILES):
+            turn(
+                [late[:, q, mt * P : (mt + 1) * P] for q in range(4)],
+                turned["x1", 1][:, mt, :, :].rearrange("m u (b i) -> m u b i", b=4),
+                "m (b i u) -> m u b i",
+            )
+            turn_back(turned["x1", 1], x_q["x1", 1][0], mt, mt + 1)
+            quantize_tiles(x_q["x1", 1], mt, mt + 1)
+
+        for mt in range(TILES):
+            e = psum.tile([P, PN], F32, name="e", tag=("h4", "h1")[mt % 2])
+            for g in range(GROUPS):
+                c1, s1 = x_q["x1", g][1:]
+                c2, s2 = x_q["x2", g][1:]
+                nc.tensor.matmul_mx(
+                    out=e[:],
+                    lhsT=c1[:, mt * P : (mt + 1) * P].bitcast(FP8X4),
+                    lhsT_scale=s1[:, mt * P : (mt + 1) * P],
+                    rhs=c2[:].bitcast(FP8X4),
+                    rhs_scale=s2[:],
+                    start=(g == 0),
+                    stop=(g == GROUPS - 1),
+                )
+            summed = work.tile([P, PN], F32, name="summed")
+            nc.vector.tensor_tensor(summed[:], e[:], pair_sb[:, mt, :], ALU.add)
+            res = work.tile([P, PN], F32, name="res", bufs=4)
+            nc.scalar.activation(res[:], summed[:], ACT.Tanh)
+            nc.sync.dma_start(out[mt * P : (mt + 1) * P, :], res[:])

@@ -22,9 +22,7 @@ PASSES = K // 512
 SLICES = H // P
 GROUPS = H // 512
 TILES = PN // P
-W1_CHUNKS = ((0, 1), (1, 2), (2, 3), (3, 4), (4, 6), (6, 8))
-W4_CHUNKS = ((0, 2), (2, 8))
-LATE_PIECES = ((0, 2), (2, 3), (3, 4))
+LATE_PIECES = ((0, 1), (1, 2), (2, 3), (3, 4))
 
 
 def tile_list_anodise_profile_dye_kernel(
@@ -42,46 +40,48 @@ def tile_list_anodise_profile_dye_kernel(
             nc.sync.dma_start(t[:], src)
             return t
 
+        rows = keep.tile([P, P], F32, name="rows")
+        nc.gpsimd.memset(rows[:], 0.0)
         ident_f32 = keep.tile([P, P], F32, name="ident_f32")
         make_identity(nc, ident_f32[:])
-        tab_sc = keep.tile([P, PASSES * T], U8, name="tab_sc")
-        nc.vector.memset(tab_sc[:].bitcast(I32), 0)
-        for q in range(4):
-            (nc.gpsimd if q < 2 else nc.scalar).dma_start(
-                tab_sc[32 * q : 32 * q + 4, :].bitcast(I32).rearrange("r (a t) -> r a t", a=PASSES),
-                tab_scales[:, 4 * q : 4 * q + 4, :].bitcast(I32).rearrange("a r t -> r a t"),
-            )
-        w4_sc = keep.tile([P, PASSES, H], U8, name="w4_sc", align_bytes=64)
-        nc.vector.memset(w4_sc[:].bitcast(I32), 0)
-        for q in range(4):
-            nc.gpsimd.dma_start(
-                w4_sc[32 * q : 32 * q + 4, :, :].bitcast(I32),
-                w4_scales[:, 4 * q : 4 * q + 4, :].bitcast(I32).rearrange("a r n -> r a n"),
-            )
-        rows = keep.tile([P, P], F32, name="rows")
-        nc.vector.memset(rows[:], 0.0)
-        for i, vec in enumerate((b1, base, rw)):
-            (nc.gpsimd if i else nc.scalar).dma_start(rows[SLICES * i : SLICES * (i + 1), :], vec.rearrange("(s p) -> s p", p=P))
         ident_bf16 = keep.tile([P, P], BF16, name="ident_bf16")
         make_identity(nc, ident_bf16[:])
+        tab_sc = keep.tile([P, PASSES * T], U8, name="tab_sc")
+        nc.vector.memset(tab_sc[:].bitcast(I32), 0)
+        nc.scalar.dma_start(
+            tab_sc[0:P:8, :].bitcast(I32).rearrange("q (a t) -> q a t", a=PASSES),
+            tab_scales.bitcast(I32).rearrange("a q t -> q a t"),
+        )
+        w4_sc = {}
+
+        def load_w4_scales(queue, s0, s1):
+            t = keep.tile([P, PASSES, (s1 - s0) * P], U8, name="w4_sc%d" % s0, align_bytes=64)
+            nc.vector.memset(t[:].bitcast(I32), 0)
+            for q in range(4):
+                queue.dma_start(
+                    t[32 * q : 32 * q + 4, :, :].bitcast(I32),
+                    w4_scales[:, 4 * q : 4 * q + 4, s0 * P : s1 * P].bitcast(I32).rearrange("a r n -> r a n"),
+                )
+            for s in range(s0, s1):
+                w4_sc[s] = t[:, :, (s - s0) * P : (s - s0 + 1) * P]
+
+        load_w4_scales(nc.scalar, 0, 2)
+        v_scales = keep.tile([P, PASSES * S], U8, name="v_scales", align_bytes=64)
+        nc.vector.memset(v_scales[:].bitcast(I32), 0)
 
         w1_raw = {}
 
-        def load_w1(c):
-            s0, s1 = W1_CHUNKS[c]
+        def load_w1(s):
             for a in range(PASSES):
-                raw = keep.tile([P, 4, (s1 - s0) * P], F32, name="w1_raw%d_%d" % (c, a))
-                nc.sync.dma_start(
-                    raw[:], w1[512 * a : 512 * (a + 1), s0 * P : s1 * P].rearrange("(p j) c -> p j c", j=4)
-                )
-                for s in range(s0, s1):
-                    w1_raw[s, a] = raw[:, :, (s - s0) * P : (s - s0 + 1) * P]
+                tag = "raw_last%d" % s if a == PASSES - 1 else "raw%d_%d" % (a, s % 4)
+                raw = keep.tile([P, 4, P], F32, name="w1_raw", tag=tag)
+                nc.sync.dma_start(raw[:], w1[512 * a : 512 * (a + 1), s * P : (s + 1) * P].rearrange("(p j) c -> p j c", j=4))
+                w1_raw[s, a] = raw
 
         w4_codes = {}
 
-        def load_w4(c):
-            s0, s1 = W4_CHUNKS[c]
-            t = keep.tile([P, PASSES, (s1 - s0) * 2 * P], U8, name="w4_codes%d" % c, align_bytes=64)
+        def load_w4(s0, s1):
+            t = keep.tile([P, PASSES, (s1 - s0) * 2 * P], U8, name="w4_codes%d" % s0, align_bytes=64)
             nc.sync.dma_start(
                 t[:].bitcast(I32),
                 w4_words[:, :, s0 * 2 * P : s1 * 2 * P].bitcast(I32).rearrange("a p n -> p a n"),
@@ -97,10 +97,11 @@ def tile_list_anodise_profile_dye_kernel(
             pages[s] = t
 
         idx = load_list(offs, "idx")
+        for i, vec in enumerate((b1, base, rw)):
+            nc.sync.dma_start(rows[SLICES * i : SLICES * (i + 1), :], vec.rearrange("(s p) -> s p", p=P))
+        load_w4(0, 1)
         idx2 = load_list(offs2, "idx2")
         idx4 = load_list(offs4, "idx4")
-        idx3 = load_list(offs3, "idx3")
-        load_w4(0)
         tab = []
         for a in range(PASSES):
             t = keep.tile([P, T], U32, name="tab%d" % a)
@@ -111,54 +112,63 @@ def tile_list_anodise_profile_dye_kernel(
         wgs_sb = keep.tile([P, S], F32, name="wgs_sb")
         nc.sync.dma_start(wgs_sb[:], wgs)
         load_w1(1)
+        idx3 = load_list(offs3, "idx3")
+        load_w4(1, 4)
         load_w1(2)
         load_page(1)
-        load_w4(1)
+        load_w4_scales(nc.sync, 2, SLICES)
         load_w1(3)
         load_page(2)
-        load_w1(4)
-        load_page(3)
-        load_page(4)
-        load_w1(5)
-        for s in range(5, SLICES):
-            load_page(s)
-        pair_sb = keep.tile([P, TILES, PN], F32, name="pair_sb")
-        nc.sync.dma_start(pair_sb[:], pair.rearrange("(t p) j -> p t j", p=P))
+        load_w4(4, 8)
 
         cols_ps = psum.tile([P, 4, P], F32, name="t2")
         nc.tensor.transpose(cols_ps[:, 0, :], rows[:], ident_f32[:])
         cols = keep.tile([P, 3 * SLICES], F32, name="cols")
         nc.scalar.copy(cols[:], cols_ps[:, 0, 0 : 3 * SLICES])
 
-        v_codes = []
-        v_scales = []
+        picked_sc = keep.tile([P, PASSES * S], U8, name="picked_sc")
         for a in range(PASSES):
-            sc = keep.tile([P, S], U8, name="v_scales%d" % a, align_bytes=64)
-            nc.vector.tensor_copy(sc[:], tab_sc[:, a * T : (a + 1) * T].indirect(idx[:]))
-            v_scales.append(sc)
+            nc.vector.tensor_copy(picked_sc[:, a * S : (a + 1) * S], tab_sc[:, a * T : (a + 1) * T].indirect(idx[:]))
+        for q in range(4):
+            nc.scalar.dma_start(
+                v_scales[32 * q : 32 * q + 4, :].bitcast(I32), picked_sc[32 * q : 32 * q + 32 : 8, :].bitcast(I32)
+            )
+        v_codes = []
+        for a in range(PASSES):
             t = keep.tile([P, S], U32, name="v_codes%d" % a, align_bytes=64)
             nc.vector.tensor_copy(t[:], tab[a][:].indirect(idx[:]))
             v_codes.append(t)
 
+        w1_bf = {}
         w1_q = {}
 
-        def quantize_w1(s, by_pass):
-            grouped = keep.tile([P, PASSES * P * 4], BF16, name="w1_bf", tag="w1_bf%d" % (s % 4), align_bytes=64)
-            codes = keep.tile([P, PASSES * P], U32, name="w1_codes%d" % s, align_bytes=64)
-            scales = keep.tile([P, PASSES * P], U8, name="w1_scales%d" % s, align_bytes=64)
+        def round_w1(s):
+            grouped = keep.tile([P, PASSES * P * 4], BF16, name="w1_bf", tag="w1_bf%d" % (s % 3), align_bytes=64)
             for a in range(PASSES):
-                part = grouped[:, a * 4 * P : (a + 1) * 4 * P]
                 nc.scalar.copy(
-                    part.rearrange("p (c i j) -> p c j i", i=4, j=4),
-                    w1_raw[s, a].rearrange("p j (c i) -> p c j i", i=4),
+                    grouped[:, a * 4 * P : (a + 1) * 4 * P].rearrange("p (c j) -> p c j", j=4),
+                    w1_raw[s, a][:].rearrange("p j c -> p c j"),
                 )
-                if by_pass:
-                    nc.vector.quantize_mx(
-                        out=codes[:, a * P : (a + 1) * P].bitcast(FP8X4), scales=scales[:, a * P : (a + 1) * P], in_=part
-                    )
-            if not by_pass:
-                nc.vector.quantize_mx(out=codes[:].bitcast(FP8X4), scales=scales[:], in_=grouped[:])
+            w1_bf[s] = grouped
+
+        def quantize_w1(s, parts):
+            codes = keep.tile([P, PASSES * P], U32, name="w1_codes", tag="w1_codes%d" % (s % 4), align_bytes=64)
+            scales = keep.tile([P, PASSES * P], U8, name="w1_scales", tag="w1_scales%d" % (s % 4), align_bytes=64)
+            width = PASSES * P // parts
+            for i in range(parts):
+                nc.vector.quantize_mx(
+                    out=codes[:, i * width : (i + 1) * width].bitcast(FP8X4),
+                    scales=scales[:, i * width : (i + 1) * width],
+                    in_=w1_bf[s][:, i * 4 * width : (i + 1) * 4 * width],
+                )
             w1_q[s] = (codes, scales)
+
+        held = {}
+
+        def held_tile(s):
+            if s not in held:
+                held[s] = keep.tile([P, S + PN + PN // 2], F32, name="held", tag="raw_last%d" % s)
+            return held[s]
 
         h_sb = {}
 
@@ -170,9 +180,9 @@ def tile_list_anodise_profile_dye_kernel(
                 nc.tensor.matmul_mx(
                     out=h4[:],
                     lhsT=w4_codes[s][:, a, :].bitcast(FP4X4),
-                    lhsT_scale=w4_sc[:, a, s * P : (s + 1) * P],
+                    lhsT_scale=w4_sc[s][:, a, :],
                     rhs=v_codes[a][:].bitcast(FP8X4),
-                    rhs_scale=v_scales[a][:],
+                    rhs_scale=v_scales[:, a * S : (a + 1) * S],
                     start=(a == 0),
                     stop=(a == PASSES - 1),
                 )
@@ -182,61 +192,62 @@ def tile_list_anodise_profile_dye_kernel(
                     lhsT=codes[:, a * P : (a + 1) * P].bitcast(FP8X4),
                     lhsT_scale=scales[:, a * P : (a + 1) * P],
                     rhs=v_codes[a][:].bitcast(FP8X4),
-                    rhs_scale=v_scales[a][:],
+                    rhs_scale=v_scales[:, a * S : (a + 1) * S],
                     start=(a == 0),
                     stop=(a == PASSES - 1),
                 )
-            h4_sb = keep.tile([P, S], F32, name="h4_sb", tag="h4_sb%d" % (s % 4))
+            h4_sb = keep.tile([P, S], F32, name="h4_sb", tag="h4_sb%d" % (s % 2), align_bytes=64)
             nc.scalar.copy(h4_sb[:], h4[:])
-            h_tag = "w1_bf%d" % ((s + 1) % 4) if 0 < s < SLICES - 1 else "h%d" % s
-            h = keep.tile([P, S], F32, name="h", tag=h_tag, align_bytes=64)
-            nc.vector.scalar_tensor_tensor(h[:], h1[:], cols[:, s : s + 1], h4_sb[:], ALU.add, ALU.max)
+            h = held_tile(s + 1 if s > 0 else 0)[:, 0:S]
+            nc.vector.scalar_tensor_tensor(h, h1[:], cols[:, s : s + 1], h4_sb[:], ALU.add, ALU.max)
             h_sb[s] = h
 
         def scatter(s):
-            nc.vector.tensor_tensor(pages[s][:].indirect(idx2[:]), h_sb[s][:], wgs_sb[:], ALU.mult)
+            nc.vector.tensor_tensor(pages[s][:].indirect(idx2[:]), h_sb[s], wgs_sb[:], ALU.mult)
 
-        def turn(blocks, dst, pattern):
-            ps = psum.tile([P, 4 * P], BF16, name="t1")
+        def turn(blocks, dst, pattern, bank):
+            ps = psum.tile([P, 4 * P], BF16, name="t1", tag="t1_%d" % bank, bufs=1)
             for i, block in enumerate(blocks):
                 nc.tensor.transpose(ps[:, i * P : (i + 1) * P], block, ident_bf16[:])
-            nc.scalar.copy(dst, ps[:].bitcast(F32).rearrange(pattern, b=4, u=2))
+            nc.scalar.copy(dst, ps[:, 0 : len(blocks) * P].bitcast(F32).rearrange(pattern, b=len(blocks), u=2))
 
         turned = {}
 
-        def turn_slice(x, name, s):
+        def turn_slice(x, name, s, bank, t0, t1):
             g, q = divmod(s, 4)
-            if q == 0:
-                turned[name, g] = keep.tile([P, TILES, 2, P], F32, name="turned_%s%d" % (name, g))
+            if (name, g) not in turned:
+                turned[name, g] = keep.tile([P, TILES, 2, P], F32, name="turned", tag="turned_" + name)
             turn(
-                [x[:, mt * P : (mt + 1) * P] for mt in range(TILES)],
-                turned[name, g][:, :, :, 32 * q : 32 * (q + 1)],
+                [x[:, mt * P : (mt + 1) * P] for mt in range(t0, t1)],
+                turned[name, g][:, t0:t1, :, 32 * q : 32 * (q + 1)],
                 "m (b i u) -> m b u i",
+                bank,
             )
 
         def fetch(s):
-            if s == 0:
-                both = keep.tile([P, PN + PN // 2], F32, name="both", tag="w1_bf1", align_bytes=64)
-            else:
-                both = keep.tile([P, PN + PN // 2], F32, name="both", tag="h4_sb%d" % ((s + 1) % 4))
-            dye = both[:, 0:PN]
-            nc.vector.tensor_copy(dye, pages[s][:].indirect(idx4[:]))
+            both = held_tile(s + 2 if s > 0 else 1)
+            dye = both[:, S : S + PN]
+            pieces = ((0, 2), (2, 4)) if s == SLICES - 1 else ((0, 4),)
+            for t0, t1 in pieces:
+                nc.vector.tensor_copy(dye[:, t0 * P : t1 * P], pages[s][:].indirect(idx4[:, t0 * 8 : t1 * 8]))
             early = s < 4
             if early:
-                x1 = both[:, PN:].bitcast(BF16)
+                x1 = both[:, S + PN :].bitcast(BF16)
                 nc.vector.tensor_copy(x1, pages[s][:].indirect(idx3[:]))
             dist = work.tile([P, PN], F32, name="dist")
-            nc.scalar.activation(dist[:], dye, ACT.Abs, bias=cols[:, SLICES + s : SLICES + s + 1], scale=-1.0)
             x2 = work.tile([P, PN], BF16, name="x2")
-            nc.scalar.activation(x2[:], dist[:], ACT.Copy, scale=cols[:, 2 * SLICES + s : 2 * SLICES + s + 1])
-            turn_slice(x2, "x2", s)
+            for i, (t0, t1) in enumerate(pieces):
+                c = slice(t0 * P, t1 * P)
+                nc.scalar.activation(dist[:, c], dye[:, c], ACT.Abs, bias=cols[:, SLICES + s : SLICES + s + 1], scale=-1.0)
+                nc.scalar.activation(x2[:, c], dist[:, c], ACT.Copy, scale=cols[:, 2 * SLICES + s : 2 * SLICES + s + 1])
+                turn_slice(x2, "x2", s, 0 if early else (s + 1 + i) % 2, t0, t1)
             if early:
-                turn_slice(x1, "x1", s)
+                turn_slice(x1, "x1", s, 1, 0, TILES)
 
-        def operand(name):
-            grouped = keep.tile([P, PN * 4], BF16, name="grouped_" + name, tag="grouped_" + name[:2], align_bytes=64)
-            codes = keep.tile([P, PN], U32, name="codes_" + name, align_bytes=64)
-            scales = keep.tile([P, PN], U8, name="scales_" + name, align_bytes=64)
+        def operand(name, g):
+            grouped = keep.tile([P, PN * 4], BF16, name="grouped", tag="grouped_" + name, align_bytes=64)
+            codes = keep.tile([P, PN], U32, name="codes_%s%d" % (name, g), align_bytes=64)
+            scales = keep.tile([P, PN], U8, name="scales_%s%d" % (name, g), align_bytes=64)
             return grouped, codes, scales
 
         def turn_back(src, grouped, t0, t1):
@@ -261,26 +272,40 @@ def tile_list_anodise_profile_dye_kernel(
         x_q = {}
 
         def quantize_x(name, g):
-            op = operand("%s%d" % (name, g))
+            op = operand(name, g)
             for half in range(2):
                 turn_back(turned[name, g], op[0], 2 * half, 2 * half + 2)
             quantize_tiles(op, 0, TILES)
             x_q[name, g] = op
 
-        quantize_w1(0, True)
+        round_w1(0)
+        quantize_w1(0, PASSES)
         make_h(0)
 
         scatter(0)
-        quantize_w1(1, False)
+        round_w1(1)
+        quantize_w1(1, 1)
+        round_w1(2)
+        for s in range(4, SLICES - 1):
+            load_w1(s)
+            load_page(s - 1)
         fetch(0)
-        quantize_w1(2, False)
         make_h(1)
+        quantize_w1(2, 1)
+        round_w1(3)
+        load_w1(SLICES - 1)
+        load_page(SLICES - 2)
+        load_page(SLICES - 1)
+        pair_sb = keep.tile([P, TILES, PN], F32, name="pair_sb")
+        nc.sync.dma_start(pair_sb[:], pair.rearrange("(t p) j -> p t j", p=P))
         scatter(1)
         for s in range(1, SLICES):
-            if s + 2 < SLICES:
-                quantize_w1(s + 2, False)
             if s + 1 < SLICES:
                 make_h(s + 1)
+            if s + 2 < SLICES:
+                quantize_w1(s + 2, 1)
+            if s + 3 < SLICES:
+                round_w1(s + 3)
             fetch(s)
             if s + 1 < SLICES:
                 scatter(s + 1)
@@ -288,23 +313,29 @@ def tile_list_anodise_profile_dye_kernel(
                 quantize_x("x2", 0)
                 quantize_x("x1", 0)
 
-        late = keep.tile([P, 4, PN], BF16, name="late", tag="h%d" % (SLICES - 1), align_bytes=64)
+        late = keep.tile([P, 4, PN], BF16, name="late", tag="h4_sb%d" % ((SLICES - 1) % 2), align_bytes=64)
         for t0, t1 in LATE_PIECES:
             for q in range(4):
                 nc.vector.tensor_copy(
                     late[:, q, t0 * P : t1 * P], pages[4 + q][:].indirect(idx3[:, t0 * P // 16 : t1 * P // 16])
                 )
         quantize_x("x2", 1)
-        x_q["x1", 1] = operand("x11")
-        turned["x1", 1] = keep.tile([P, TILES, 2, P], F32, name="turned_x11")
+        codes = keep.tile([P, PN], U32, name="codes_x11", tag="h4_sb%d" % ((SLICES - 1) % 2), align_bytes=64)
+        scales = keep.tile([P, PN], U8, name="scales_x11", align_bytes=64)
+        x_q["x1", 1] = (None, codes, scales)
+        turned["x1", 1] = keep.tile([P, TILES, 2, P], F32, name="turned", tag="turned_x1")
         for mt in range(TILES):
             turn(
                 [late[:, q, mt * P : (mt + 1) * P] for q in range(4)],
                 turned["x1", 1][:, mt, :, :].rearrange("m u (b i) -> m u b i", b=4),
                 "m (b i u) -> m u b i",
+                mt % 2,
             )
-            turn_back(turned["x1", 1], x_q["x1", 1][0], mt, mt + 1)
-            quantize_tiles(x_q["x1", 1], mt, mt + 1)
+            grouped = keep.tile([P, 4 * P], BF16, name="grouped", tag="last%d" % mt, align_bytes=64)
+            turn_back(turned["x1", 1][:, mt : mt + 1, :, :], grouped, 0, 1)
+            nc.vector.quantize_mx(
+                out=codes[:, mt * P : (mt + 1) * P].bitcast(FP8X4), scales=scales[:, mt * P : (mt + 1) * P], in_=grouped[:]
+            )
 
         for mt in range(TILES):
             e = psum.tile([P, PN], F32, name="e", tag=("h4", "h1")[mt % 2])
@@ -320,8 +351,8 @@ def tile_list_anodise_profile_dye_kernel(
                     start=(g == 0),
                     stop=(g == GROUPS - 1),
                 )
-            summed = work.tile([P, PN], F32, name="summed")
+            summed = work.tile([P, PN], F32, name="summed", bufs=4)
             nc.vector.tensor_tensor(summed[:], e[:], pair_sb[:, mt, :], ALU.add)
-            res = work.tile([P, PN], F32, name="res", bufs=4)
+            res = keep.tile([P, PN], F32, name="res", tag="res%d" % mt if mt else "turned_x1")
             nc.scalar.activation(res[:], summed[:], ACT.Tanh)
             nc.sync.dma_start(out[mt * P : (mt + 1) * P, :], res[:])

@@ -167,7 +167,7 @@ def tile_list_anodise_profile_dye_kernel(
 
         def held_tile(s):
             if s not in held:
-                held[s] = keep.tile([P, S + PN + PN // 2], F32, name="held", tag="raw_last%d" % s)
+                held[s] = keep.tile([P, S + PN + PN // 2 + (PN if 3 <= s < SLICES else 0)], F32, name="held", tag="raw_last%d" % s)
             return held[s]
 
         h_sb = {}
@@ -224,31 +224,31 @@ def tile_list_anodise_profile_dye_kernel(
                 bank,
             )
 
+        def pieces(s):
+            return ((0, 2), (2, 4)) if s == SLICES - 1 else ((0, 4),)
+
         def fetch(s):
             both = held_tile(s + 2 if s > 0 else 1)
+            for t0, t1 in pieces(s):
+                nc.vector.tensor_copy(both[:, S + t0 * P : S + t1 * P], pages[s][:].indirect(idx4[:, t0 * 8 : t1 * 8]))
+            if s < 4:
+                nc.vector.tensor_copy(both[:, S + PN : S + PN + PN // 2].bitcast(BF16), pages[s][:].indirect(idx3[:]))
+
+        def finish(s):
+            both = held_tile(s + 2 if s > 0 else 1)
             dye = both[:, S : S + PN]
-            pieces = ((0, 2), (2, 4)) if s == SLICES - 1 else ((0, 4),)
-            for t0, t1 in pieces:
-                nc.vector.tensor_copy(dye[:, t0 * P : t1 * P], pages[s][:].indirect(idx4[:, t0 * 8 : t1 * 8]))
-            early = s < 4
-            if early:
-                x1 = both[:, S + PN :].bitcast(BF16)
-                nc.vector.tensor_copy(x1, pages[s][:].indirect(idx3[:]))
-            dist = work.tile([P, PN], F32, name="dist")
+            if s + 3 < SLICES:
+                dist = held_tile(s + 3)[:, S + PN + PN // 2 :]
+            else:
+                dist = work.tile([P, PN], F32, name="dist")
             x2 = work.tile([P, PN], BF16, name="x2")
-            for i, (t0, t1) in enumerate(pieces):
+            for i, (t0, t1) in enumerate(pieces(s)):
                 c = slice(t0 * P, t1 * P)
                 nc.scalar.activation(dist[:, c], dye[:, c], ACT.Abs, bias=cols[:, SLICES + s : SLICES + s + 1], scale=-1.0)
                 nc.scalar.activation(x2[:, c], dist[:, c], ACT.Copy, scale=cols[:, 2 * SLICES + s : 2 * SLICES + s + 1])
-                turn_slice(x2, "x2", s, 0 if early else (s + 1 + i) % 2, t0, t1)
-            if early:
-                turn_slice(x1, "x1", s, 1, 0, TILES)
-
-        def operand(name, g):
-            grouped = keep.tile([P, PN * 4], BF16, name="grouped", tag="grouped_" + name, align_bytes=64)
-            codes = keep.tile([P, PN], U32, name="codes_%s%d" % (name, g), align_bytes=64)
-            scales = keep.tile([P, PN], U8, name="scales_%s%d" % (name, g), align_bytes=64)
-            return grouped, codes, scales
+                turn_slice(x2, "x2", s, (s + 1 + i) % 2, t0, t1)
+            if s < 4:
+                turn_slice(both[:, S + PN : S + PN + PN // 2].bitcast(BF16), "x1", s, (s + 1) % 2, 0, TILES)
 
         def turn_back(src, grouped, t0, t1):
             n = t1 - t0
@@ -261,22 +261,20 @@ def tile_list_anodise_profile_dye_kernel(
                 ps[:, 0 : 2 * n, :].rearrange("p (j u) m -> p j m u", u=2),
             )
 
-        def quantize_tiles(op, t0, t1):
-            grouped, codes, scales = op
-            nc.vector.quantize_mx(
-                out=codes[:, t0 * P : t1 * P].bitcast(FP8X4),
-                scales=scales[:, t0 * P : t1 * P],
-                in_=grouped[:, t0 * 4 * P : t1 * 4 * P],
-            )
-
+        x_bf = {}
         x_q = {}
 
-        def quantize_x(name, g):
-            op = operand(name, g)
+        def interleave_x(name, g):
+            grouped = keep.tile([P, PN * 4], BF16, name="grouped", tag="grouped_" + name, align_bytes=64)
             for half in range(2):
-                turn_back(turned[name, g], op[0], 2 * half, 2 * half + 2)
-            quantize_tiles(op, 0, TILES)
-            x_q[name, g] = op
+                turn_back(turned[name, g], grouped, 2 * half, 2 * half + 2)
+            x_bf[name, g] = grouped
+
+        def quantize_x(name, g, tag):
+            codes = keep.tile([P, PN], U32, name="x_codes", tag=tag, align_bytes=64)
+            scales = keep.tile([P, PN], U8, name="scales_%s%d" % (name, g), align_bytes=64)
+            nc.vector.quantize_mx(out=codes[:].bitcast(FP8X4), scales=scales[:], in_=x_bf[name, g][:])
+            x_q[name, g] = (codes, scales)
 
         round_w1(0)
         quantize_w1(0, PASSES)
@@ -293,10 +291,11 @@ def tile_list_anodise_profile_dye_kernel(
         make_h(1)
         quantize_w1(2, 1)
         round_w1(3)
+        finish(0)
         load_w1(SLICES - 1)
         load_page(SLICES - 2)
         load_page(SLICES - 1)
-        pair_sb = keep.tile([P, TILES, PN], F32, name="pair_sb")
+        pair_sb = keep.tile([P, TILES, PN], F32, name="pair_sb", tag="tab0")
         nc.sync.dma_start(pair_sb[:], pair.rearrange("(t p) j -> p t j", p=P))
         scatter(1)
         for s in range(1, SLICES):
@@ -307,11 +306,14 @@ def tile_list_anodise_profile_dye_kernel(
             if s + 3 < SLICES:
                 round_w1(s + 3)
             fetch(s)
+            finish(s)
             if s + 1 < SLICES:
                 scatter(s + 1)
             if s == 3:
-                quantize_x("x2", 0)
-                quantize_x("x1", 0)
+                interleave_x("x2", 0)
+                interleave_x("x1", 0)
+            if s in (5, 6):
+                quantize_x("x2" if s == 5 else "x1", 0, "w1_codes%d" % ((s + 1) % 4))
 
         late = keep.tile([P, 4, PN], BF16, name="late", tag="h4_sb%d" % ((SLICES - 1) % 2), align_bytes=64)
         for t0, t1 in LATE_PIECES:
@@ -319,17 +321,18 @@ def tile_list_anodise_profile_dye_kernel(
                 nc.vector.tensor_copy(
                     late[:, q, t0 * P : t1 * P], pages[4 + q][:].indirect(idx3[:, t0 * P // 16 : t1 * P // 16])
                 )
-        quantize_x("x2", 1)
+        interleave_x("x2", 1)
+        quantize_x("x2", 1, "x2_codes_last")
         codes = keep.tile([P, PN], U32, name="codes_x11", tag="h4_sb%d" % ((SLICES - 1) % 2), align_bytes=64)
         scales = keep.tile([P, PN], U8, name="scales_x11", align_bytes=64)
-        x_q["x1", 1] = (None, codes, scales)
+        x_q["x1", 1] = (codes, scales)
         turned["x1", 1] = keep.tile([P, TILES, 2, P], F32, name="turned", tag="turned_x1")
         for mt in range(TILES):
             turn(
                 [late[:, q, mt * P : (mt + 1) * P] for q in range(4)],
                 turned["x1", 1][:, mt, :, :].rearrange("m u (b i) -> m u b i", b=4),
                 "m (b i u) -> m u b i",
-                mt % 2,
+                1 if mt == 1 else 0,
             )
             grouped = keep.tile([P, 4 * P], BF16, name="grouped", tag="last%d" % mt, align_bytes=64)
             turn_back(turned["x1", 1][:, mt : mt + 1, :, :], grouped, 0, 1)
@@ -340,8 +343,8 @@ def tile_list_anodise_profile_dye_kernel(
         for mt in range(TILES):
             e = psum.tile([P, PN], F32, name="e", tag=("h4", "h1")[mt % 2])
             for g in range(GROUPS):
-                c1, s1 = x_q["x1", g][1:]
-                c2, s2 = x_q["x2", g][1:]
+                c1, s1 = x_q["x1", g]
+                c2, s2 = x_q["x2", g]
                 nc.tensor.matmul_mx(
                     out=e[:],
                     lhsT=c1[:, mt * P : (mt + 1) * P].bitcast(FP8X4),
@@ -351,7 +354,7 @@ def tile_list_anodise_profile_dye_kernel(
                     start=(g == 0),
                     stop=(g == GROUPS - 1),
                 )
-            summed = work.tile([P, PN], F32, name="summed", bufs=4)
+            summed = keep.tile([P, PN], F32, name="summed", tag="last3" if mt == 1 else "summed%d" % mt, align_bytes=64)
             nc.vector.tensor_tensor(summed[:], e[:], pair_sb[:, mt, :], ALU.add)
             res = keep.tile([P, PN], F32, name="res", tag="res%d" % mt if mt else "turned_x1")
             nc.scalar.activation(res[:], summed[:], ACT.Tanh)

@@ -198,7 +198,7 @@ def tile_list_anodise_profile_dye_kernel(
                 )
             h4_sb = keep.tile([P, S], F32, name="h4_sb", tag="h4_sb%d" % (s % 2), align_bytes=64)
             nc.scalar.copy(h4_sb[:], h4[:])
-            h = held_tile(s + 1 if s > 0 else 0)[:, 0:S]
+            h = held_tile(s + 1 if s > 2 else s)[:, 0:S]
             nc.vector.scalar_tensor_tensor(h, h1[:], cols[:, s : s + 1], h4_sb[:], ALU.add, ALU.max)
             h_sb[s] = h
 
@@ -228,14 +228,14 @@ def tile_list_anodise_profile_dye_kernel(
             return ((0, 2), (2, 4)) if s == SLICES - 1 else ((0, 4),)
 
         def fetch(s):
-            both = held_tile(s + 2 if s > 0 else 1)
+            both = held_tile(s + 2 if s > 2 else s + 1)
             for t0, t1 in pieces(s):
                 nc.vector.tensor_copy(both[:, S + t0 * P : S + t1 * P], pages[s][:].indirect(idx4[:, t0 * 8 : t1 * 8]))
             if s < 4:
                 nc.vector.tensor_copy(both[:, S + PN : S + PN + PN // 2].bitcast(BF16), pages[s][:].indirect(idx3[:]))
 
         def finish(s):
-            both = held_tile(s + 2 if s > 0 else 1)
+            both = held_tile(s + 2 if s > 2 else s + 1)
             dye = both[:, S : S + PN]
             if s + 3 < SLICES:
                 dist = held_tile(s + 3)[:, S + PN + PN // 2 :]
@@ -283,22 +283,34 @@ def tile_list_anodise_profile_dye_kernel(
         scatter(0)
         round_w1(1)
         quantize_w1(1, 1)
+        fetch(0)
+        make_h(1)
         round_w1(2)
         for s in range(4, SLICES - 1):
             load_w1(s)
             load_page(s - 1)
-        fetch(0)
-        make_h(1)
+        scatter(1)
         quantize_w1(2, 1)
+        fetch(1)
+        make_h(2)
         round_w1(3)
-        finish(0)
         load_w1(SLICES - 1)
         load_page(SLICES - 2)
         load_page(SLICES - 1)
         pair_sb = keep.tile([P, TILES, PN], F32, name="pair_sb", tag="tab0")
         nc.sync.dma_start(pair_sb[:], pair.rearrange("(t p) j -> p t j", p=P))
-        scatter(1)
-        for s in range(1, SLICES):
+        finish(0)
+        scatter(2)
+        quantize_w1(3, 1)
+        fetch(2)
+        round_w1(4)
+        make_h(3)
+        quantize_w1(4, 1)
+        round_w1(5)
+        finish(1)
+        finish(2)
+        scatter(3)
+        for s in range(3, SLICES):
             if s + 1 < SLICES:
                 make_h(s + 1)
             if s + 2 < SLICES:
@@ -332,7 +344,7 @@ def tile_list_anodise_profile_dye_kernel(
                 [late[:, q, mt * P : (mt + 1) * P] for q in range(4)],
                 turned["x1", 1][:, mt, :, :].rearrange("m u (b i) -> m u b i", b=4),
                 "m (b i u) -> m u b i",
-                1 if mt == 1 else 0,
+                mt % 2,
             )
             grouped = keep.tile([P, 4 * P], BF16, name="grouped", tag="last%d" % mt, align_bytes=64)
             turn_back(turned["x1", 1][:, mt : mt + 1, :, :], grouped, 0, 1)

from contextlib import ExitStack

import concourse.mybir as mybir
from concourse.masks import make_identity

K, H, T, S, T2, PN = 1536, 1024, 2048, 512, 1024, 512
FLOPS = 2 * (2 * K * H * S + H * PN * PN)

F32 = mybir.dt.float32
BF16 = mybir.dt.bfloat16
I32 = mybir.dt.int32
U32 = mybir.dt.uint32
U16 = mybir.dt.uint16
U8 = mybir.dt.uint8
FP8X4 = mybir.dt.float8_e4m3fn_x4
FP4X4 = mybir.dt.float4_e2m1fn_x4
ALU = mybir.AluOpType
ACT = mybir.ActivationFunctionType

P = 128
PASSES = K // 512
SLICES = H // P
GROUPS = H // 512
TILES = PN // P
LATE_PIECES = ((0, 1), (1, 2), (2, 3), (3, 4))


def tile_list_anodise_profile_dye_kernel(
    tc, tab_words, tab_scales, offs, w1, b1, w4_words, w4_scales, page0, wgs, offs2, offs3, offs4, base, rw, pair, out
):
    nc = tc.nc
    with ExitStack() as ctx:
        lists = ctx.enter_context(tc.tile_pool(name="lists", bufs=1))
        keep = ctx.enter_context(tc.tile_pool(name="keep", bufs=1))
        work = ctx.enter_context(tc.tile_pool(name="work", bufs=2))
        psum = ctx.enter_context(tc.psum_pool(name="psum", bufs=2))

        def load_list(src, name):
            t = lists.tile([P, S // 16], U16, name=name)
            nc.sync.dma_start(t[:], src)
            return t

        rows = keep.tile([P, P], F32, name="rows")
        nc.gpsimd.memset(rows[:], 0.0)
        ident_f32 = keep.tile([P, P], F32, name="ident_f32")
        make_identity(nc, ident_f32[:])
        ident_bf16 = keep.tile([P, P], BF16, name="ident_bf16")
        make_identity(nc, ident_bf16[:])
        tab_sc = keep.tile([P, PASSES * T], U8, name="tab_sc")
        nc.vector.memset(tab_sc[:].bitcast(I32), 0)
        nc.scalar.dma_start(
            tab_sc[0:P:8, :].bitcast(I32).rearrange("q (a t) -> q a t", a=PASSES),
            tab_scales.bitcast(I32).rearrange("a q t -> q a t"),
        )
        w4_sc = {}

        def load_w4_scales(queue, s0, s1):
            t = keep.tile([P, PASSES, (s1 - s0) * P], U8, name="w4_sc%d" % s0, align_bytes=64)
            nc.vector.memset(t[:].bitcast(I32), 0)
            for q in range(4):
                queue.dma_start(
                    t[32 * q : 32 * q + 4, :, :].bitcast(I32),
                    w4_scales[:, 4 * q : 4 * q + 4, s0 * P : s1 * P].bitcast(I32).rearrange("a r n -> r a n"),
                )
            for s in range(s0, s1):
                w4_sc[s] = t[:, :, (s - s0) * P : (s - s0 + 1) * P]

        load_w4_scales(nc.scalar, 0, 2)
        v_scales = keep.tile([P, PASSES * S], U8, name="v_scales", align_bytes=64)
        nc.vector.memset(v_scales[:].bitcast(I32), 0)

        w1_raw = {}

        def load_w1(s):
            for a in range(PASSES):
                tag = "raw_last%d" % s if a == PASSES - 1 else "raw%d_%d" % (a, s % 4)
                raw = keep.tile([P, 4, P], F32, name="w1_raw", tag=tag)
                nc.sync.dma_start(raw[:], w1[512 * a : 512 * (a + 1), s * P : (s + 1) * P].rearrange("(p j) c -> p j c", j=4))
                w1_raw[s, a] = raw

        w4_codes = {}

        def load_w4(s0, s1):
            t = keep.tile([P, PASSES, (s1 - s0) * 2 * P], U8, name="w4_codes%d" % s0, align_bytes=64)
            nc.sync.dma_start(
                t[:].bitcast(I32),
                w4_words[:, :, s0 * 2 * P : s1 * 2 * P].bitcast(I32).rearrange("a p n -> p a n"),
            )
            for s in range(s0, s1):
                w4_codes[s] = t[:, :, (s - s0) * 2 * P : (s - s0 + 1) * 2 * P]

        pages = {}

        def load_page(s):
            t = keep.tile([P, T2], F32, name="page%d" % s)
            nc.sync.dma_start(t[:], page0[s * P : (s + 1) * P, :])
            pages[s] = t

        idx = load_list(offs, "idx")
        for i, vec in enumerate((b1, base, rw)):
            nc.sync.dma_start(rows[SLICES * i : SLICES * (i + 1), :], vec.rearrange("(s p) -> s p", p=P))
        load_w4(0, 1)
        idx2 = load_list(offs2, "idx2")
        idx4 = load_list(offs4, "idx4")
        tab = []
        for a in range(PASSES):
            t = keep.tile([P, T], U32, name="tab%d" % a)
            nc.sync.dma_start(t[:].bitcast(I32), tab_words[a].rearrange("p t i -> p (t i)").bitcast(I32))
            tab.append(t)
        load_w1(0)
        load_page(0)
        wgs_sb = keep.tile([P, S], F32, name="wgs_sb")
        nc.sync.dma_start(wgs_sb[:], wgs)
        load_w1(1)
        idx3 = load_list(offs3, "idx3")
        load_w4(1, 4)
        load_w1(2)
        load_page(1)
        load_w4_scales(nc.sync, 2, SLICES)
        load_w1(3)
        load_page(2)
        load_w4(4, 8)

        cols_ps = psum.tile([P, 4, P], F32, name="t2")
        nc.tensor.transpose(cols_ps[:, 0, :], rows[:], ident_f32[:])
        cols = keep.tile([P, 3 * SLICES], F32, name="cols")
        nc.scalar.copy(cols[:], cols_ps[:, 0, 0 : 3 * SLICES])

        picked_sc = keep.tile([P, PASSES * S], U8, name="picked_sc")
        for a in range(PASSES):
            nc.vector.tensor_copy(picked_sc[:, a * S : (a + 1) * S], tab_sc[:, a * T : (a + 1) * T].indirect(idx[:]))
        for q in range(4):
            nc.scalar.dma_start(
                v_scales[32 * q : 32 * q + 4, :].bitcast(I32), picked_sc[32 * q : 32 * q + 32 : 8, :].bitcast(I32)
            )
        v_codes = []
        for a in range(PASSES):
            t = keep.tile([P, S], U32, name="v_codes%d" % a, align_bytes=64)
            nc.vector.tensor_copy(t[:], tab[a][:].indirect(idx[:]))
            v_codes.append(t)

        w1_bf = {}
        w1_q = {}

        def round_w1(s):
            grouped = keep.tile([P, PASSES * P * 4], BF16, name="w1_bf", tag="w1_bf%d" % (s % 3), align_bytes=64)
            for a in range(PASSES):
                nc.scalar.copy(
                    grouped[:, a * 4 * P : (a + 1) * 4 * P].rearrange("p (c j) -> p c j", j=4),
                    w1_raw[s, a][:].rearrange("p j c -> p c j"),
                )
            w1_bf[s] = grouped

        def quantize_w1(s, parts):
            codes = keep.tile([P, PASSES * P], U32, name="w1_codes", tag="w1_codes%d" % (s % 4), align_bytes=64)
            scales = keep.tile([P, PASSES * P], U8, name="w1_scales", tag="w1_scales%d" % (s % 4), align_bytes=64)
            width = PASSES * P // parts
            for i in range(parts):
                nc.vector.quantize_mx(
                    out=codes[:, i * width : (i + 1) * width].bitcast(FP8X4),
                    scales=scales[:, i * width : (i + 1) * width],
                    in_=w1_bf[s][:, i * 4 * width : (i + 1) * 4 * width],
                )
            w1_q[s] = (codes, scales)

        held = {}

        def held_tile(s):
            if s not in held:
                held[s] = keep.tile([P, S + PN + PN // 2 + (PN if 3 <= s < SLICES else 0)], F32, name="held", tag="raw_last%d" % s)
            return held[s]

        h_sb = {}

        def make_h(s):
            h4 = psum.tile([P, S], F32, name="h4")
            h1 = psum.tile([P, S], F32, name="h1")
            codes, scales = w1_q[s]
            for a in range(PASSES):
                nc.tensor.matmul_mx(
                    out=h4[:],
                    lhsT=w4_codes[s][:, a, :].bitcast(FP4X4),
                    lhsT_scale=w4_sc[s][:, a, :],
                    rhs=v_codes[a][:].bitcast(FP8X4),
                    rhs_scale=v_scales[:, a * S : (a + 1) * S],
                    start=(a == 0),
                    stop=(a == PASSES - 1),
                )
            for a in range(PASSES):
                nc.tensor.matmul_mx(
                    out=h1[:],
                    lhsT=codes[:, a * P : (a + 1) * P].bitcast(FP8X4),
                    lhsT_scale=scales[:, a * P : (a + 1) * P],
                    rhs=v_codes[a][:].bitcast(FP8X4),
                    rhs_scale=v_scales[:, a * S : (a + 1) * S],
                    start=(a == 0),
                    stop=(a == PASSES - 1),
                )
            h4_sb = keep.tile([P, S], F32, name="h4_sb", tag="h4_sb%d" % (s % 2), align_bytes=64)
            nc.scalar.copy(h4_sb[:], h4[:])
            h = held_tile(s + 1 if s > 2 else s)[:, 0:S]
            nc.vector.scalar_tensor_tensor(h, h1[:], cols[:, s : s + 1], h4_sb[:], ALU.add, ALU.max)
            h_sb[s] = h

        def scatter(s):
            nc.vector.tensor_tensor(pages[s][:].indirect(idx2[:]), h_sb[s], wgs_sb[:], ALU.mult)

        def turn(blocks, dst, pattern, bank):
            ps = psum.tile([P, 4 * P], BF16, name="t1", tag="t1_%d" % bank, bufs=1)
            for i, block in enumerate(blocks):
                nc.tensor.transpose(ps[:, i * P : (i + 1) * P], block, ident_bf16[:])
            nc.scalar.copy(dst, ps[:, 0 : len(blocks) * P].bitcast(F32).rearrange(pattern, b=len(blocks), u=2))

        turned = {}

        def turn_slice(x, name, s, bank, t0, t1):
            g, q = divmod(s, 4)
            if (name, g) not in turned:
                turned[name, g] = keep.tile([P, TILES, 2, P], F32, name="turned", tag="turned_" + name)
            turn(
                [x[:, mt * P : (mt + 1) * P] for mt in range(t0, t1)],
                turned[name, g][:, t0:t1, :, 32 * q : 32 * (q + 1)],
                "m (b i u) -> m b u i",
                bank,
            )

        def pieces(s):
            return ((0, 2), (2, 4)) if s == SLICES - 1 else ((0, 4),)

        def fetch(s):
            both = held_tile(s + 2 if s > 2 else s + 1)
            for t0, t1 in pieces(s):
                nc.vector.tensor_copy(both[:, S + t0 * P : S + t1 * P], pages[s][:].indirect(idx4[:, t0 * 8 : t1 * 8]))
            if s < 4:
                nc.vector.tensor_copy(both[:, S + PN : S + PN + PN // 2].bitcast(BF16), pages[s][:].indirect(idx3[:]))

        def finish(s):
            both = held_tile(s + 2 if s > 2 else s + 1)
            dye = both[:, S : S + PN]
            if s + 3 < SLICES:
                dist = held_tile(s + 3)[:, S + PN + PN // 2 :]
            else:
                dist = work.tile([P, PN], F32, name="dist")
            x2 = work.tile([P, PN], BF16, name="x2")
            for i, (t0, t1) in enumerate(pieces(s)):
                c = slice(t0 * P, t1 * P)
                nc.scalar.activation(dist[:, c], dye[:, c], ACT.Abs, bias=cols[:, SLICES + s : SLICES + s + 1], scale=-1.0)
                nc.scalar.activation(x2[:, c], dist[:, c], ACT.Copy, scale=cols[:, 2 * SLICES + s : 2 * SLICES + s + 1])
                turn_slice(x2, "x2", s, (s + 1 + i) % 2, t0, t1)
            if s < 4:
                turn_slice(both[:, S + PN : S + PN + PN // 2].bitcast(BF16), "x1", s, (s + 1) % 2, 0, TILES)

        def turn_back(src, grouped, t0, t1):
            n = t1 - t0
            ps = psum.tile([P, 4, P], F32, name="t2")
            for j in range(n):
                for u in range(2):
                    nc.tensor.transpose(ps[:, 2 * j + u, :], src[:, t0 + j, u, :], ident_f32[:])
            nc.scalar.copy(
                grouped[:, t0 * 4 * P : t1 * 4 * P].bitcast(F32).rearrange("p (j m u) -> p j m u", j=n, u=2),
                ps[:, 0 : 2 * n, :].rearrange("p (j u) m -> p j m u", u=2),
            )

        x_bf = {}
        x_q = {}

        def interleave_x(name, g):
            grouped = keep.tile([P, PN * 4], BF16, name="grouped", tag="grouped_" + name, align_bytes=64)
            for half in range(2):
                turn_back(turned[name, g], grouped, 2 * half, 2 * half + 2)
            x_bf[name, g] = grouped

        def quantize_x(name, g, tag):
            codes = keep.tile([P, PN], U32, name="x_codes", tag=tag, align_bytes=64)
            scales = keep.tile([P, PN], U8, name="scales_%s%d" % (name, g), align_bytes=64)
            nc.vector.quantize_mx(out=codes[:].bitcast(FP8X4), scales=scales[:], in_=x_bf[name, g][:])
            x_q[name, g] = (codes, scales)

        round_w1(0)
        quantize_w1(0, PASSES)
        make_h(0)

        scatter(0)
        round_w1(1)
        quantize_w1(1, 1)
        fetch(0)
        make_h(1)
        round_w1(2)
        for s in range(4, SLICES - 1):
            load_w1(s)
            load_page(s - 1)
        scatter(1)
        quantize_w1(2, 1)
        fetch(1)
        make_h(2)
        round_w1(3)
        load_w1(SLICES - 1)
        load_page(SLICES - 2)
        load_page(SLICES - 1)
        pair_sb = keep.tile([P, TILES, PN], F32, name="pair_sb", tag="tab0")
        nc.sync.dma_start(pair_sb[:], pair.rearrange("(t p) j -> p t j", p=P))
        finish(0)
        scatter(2)
        quantize_w1(3, 1)
        fetch(2)
        round_w1(4)
        make_h(3)
        quantize_w1(4, 1)
        round_w1(5)
        finish(1)
        finish(2)
        scatter(3)
        for s in range(3, SLICES):
            if s + 1 < SLICES:
                make_h(s + 1)
            if s + 2 < SLICES:
                quantize_w1(s + 2, 1)
            if s + 3 < SLICES:
                round_w1(s + 3)
            fetch(s)
            finish(s)
            if s + 1 < SLICES:
                scatter(s + 1)
            if s == 3:
                interleave_x("x2", 0)
                interleave_x("x1", 0)
            if s in (5, 6):
                quantize_x("x2" if s == 5 else "x1", 0, "w1_codes%d" % ((s + 1) % 4))

        late = keep.tile([P, 4, PN], BF16, name="late", tag="h4_sb%d" % ((SLICES - 1) % 2), align_bytes=64)
        for t0, t1 in LATE_PIECES:
            for q in range(4):
                nc.vector.tensor_copy(
                    late[:, q, t0 * P : t1 * P], pages[4 + q][:].indirect(idx3[:, t0 * P // 16 : t1 * P // 16])
                )
        interleave_x("x2", 1)
        quantize_x("x2", 1, "x2_codes_last")
        codes = keep.tile([P, PN], U32, name="codes_x11", tag="h4_sb%d" % ((SLICES - 1) % 2), align_bytes=64)
        scales = keep.tile([P, PN], U8, name="scales_x11", align_bytes=64)
        x_q["x1", 1] = (codes, scales)
        turned["x1", 1] = keep.tile([P, TILES, 2, P], F32, name="turned", tag="turned_x1")
        for mt in range(TILES):
            turn(
                [late[:, q, mt * P : (mt + 1) * P] for q in range(4)],
                turned["x1", 1][:, mt, :, :].rearrange("m u (b i) -> m u b i", b=4),
                "m (b i u) -> m u b i",
                mt % 2,
            )
            grouped = keep.tile([P, 4 * P], BF16, name="grouped", tag="last%d" % mt, align_bytes=64)
            turn_back(turned["x1", 1][:, mt : mt + 1, :, :], grouped, 0, 1)
            nc.vector.quantize_mx(
                out=codes[:, mt * P : (mt + 1) * P].bitcast(FP8X4), scales=scales[:, mt * P : (mt + 1) * P], in_=grouped[:]
            )

        for mt in range(TILES):
            e = psum.tile([P, PN], F32, name="e", tag=("h4", "h1")[mt % 2])
            for g in range(GROUPS):
                c1, s1 = x_q["x1", g]
                c2, s2 = x_q["x2", g]
                nc.tensor.matmul_mx(
                    out=e[:],
                    lhsT=c1[:, mt * P : (mt + 1) * P].bitcast(FP8X4),
                    lhsT_scale=s1[:, mt * P : (mt + 1) * P],
                    rhs=c2[:].bitcast(FP8X4),
                    rhs_scale=s2[:],
                    start=(g == 0),
                    stop=(g == GROUPS - 1),
                )
            summed = keep.tile([P, PN], F32, name="summed", tag="last3" if mt == 1 else "summed%d" % mt, align_bytes=64)
            nc.vector.tensor_tensor(summed[:], e[:], pair_sb[:, mt, :], ALU.add)
            res = keep.tile([P, PN], F32, name="res", tag="res%d" % mt if mt else "turned_x1")
            nc.scalar.activation(res[:], summed[:], ACT.Tanh)
            nc.sync.dma_start(out[mt * P : (mt + 1) * P, :], res[:])
